import numpy as np
import ml_dtypes


def mxq(x, axis, fmt="e4m3"):
    dtype, down = {"e4m3": (ml_dtypes.float8_e4m3fn, 7), "e5m2": (ml_dtypes.float8_e5m2, 14)}[fmt]
    v = np.moveaxis(np.asarray(x, np.float32).astype(ml_dtypes.bfloat16).astype(np.float64), axis, -1)
    blocks = v.reshape(v.shape[:-1] + (-1, 32))
    amax = np.abs(blocks).max(-1, keepdims=True)
    byte = np.maximum(np.where(amax > 0, np.frexp(amax)[1] - 1 + 127, 0) - down, 1)
    scale = np.exp2(byte - 127.0)
    codes = (blocks / scale).astype(np.float32).astype(dtype).astype(np.float64)
    return np.moveaxis((codes * scale).reshape(v.shape), -1, axis)


WIDE = False


def mx_kscale(k):
    if not WIDE:
        return np.ones(k)
    levels = np.array([10, -10, 5, -5, 0])
    if k % 512:
        return np.exp2(np.random.permutation(np.resize(levels, k // 32))).repeat(32)
    a = np.empty((k // 512, 16))
    for p in range(k // 512):
        a[p, :8] = np.random.permutation(np.resize(levels, 8))
        for g in range(8):
            far = levels[np.abs(levels - a[p, g]) >= 10]
            a[p, g + 8] = far[np.random.randint(len(far))]
    return np.exp2(a.ravel()).repeat(32)


def f64(x):
    return np.asarray(x).astype(np.float64)


def striped(idx):
    return np.tile(idx.reshape(-1, 16).T, (8, 1)).astype(np.uint16)


def unstriped(offs):
    return offs[:16].T.reshape(-1).astype(np.int64)


def pack_weight(w):
    k, n = w.shape
    w = f64(np.asarray(w, np.float32).astype(ml_dtypes.bfloat16)).reshape(k // 32, 32, n)
    amax = np.abs(w).max(1)
    byte = np.clip(np.where(amax > 0, np.frexp(amax)[1] - 1 + 127 - 7, 1), 1, 254)
    scaled = (w * np.exp2(127.0 - byte)[:, None, :]).reshape(k, n).astype(np.float32)
    words = np.ascontiguousarray(scaled.reshape(k // 512, 128, 4, n).transpose(0, 1, 3, 2)).astype(ml_dtypes.float8_e4m3fn).view(np.uint8)
    return words, np.ascontiguousarray(byte.astype(np.uint8).reshape(k // 512, 16, n))


def unpack_weight(words, scales):
    g, p, n, _ = words.shape
    vals = np.ascontiguousarray(words).view(ml_dtypes.float8_e4m3fn).astype(np.float64) * np.repeat(np.exp2(scales.astype(np.float64) - 127.0), 8, axis=1)[..., None]
    return vals.transpose(0, 1, 3, 2).reshape(g * 512, n)


K, T, S, N, H = 512, 1024, 512, 128, 512


def setup_inputs():
    n = np.random.standard_normal
    s = mx_kscale(K)[:, None]
    u = mx_kscale(H)
    packed_xT = pack_weight(n((K, T)) * s)
    return {
        "x_words": packed_xT[0],
        "x_scales": packed_xT[1],
        "w1": (n((K, H)) / np.sqrt(K) / s).astype(np.float32),
        "dir_": (np.random.uniform(0.1, 0.9, (H, S))).astype(np.float32),
        "unit": (np.random.uniform(0.6, 1.4, (H, 1)) * u[:, None]).astype(np.float32),
        "w2": (n((H, N)) / np.sqrt(H) / u[:, None]).astype(np.float32),
        "offs": striped(np.random.permutation(T)[:S]),
        "c1": striped(np.random.permutation(S)),
        "c2": striped(np.random.permutation(S)),
    }


def reference(x_words, x_scales, w1, dir_, unit, w2, offs, c1, c2):
    xq = unpack_weight(x_words, x_scales)[:, unstriped(offs)]
    y = mxq(f64(w1), 0, "e4m3").T @ xq
    yp = y[:, unstriped(c1)]
    lo = np.minimum(y, yp)
    hi = np.maximum(y, yp)
    stg = f64(dir_) * lo + (-1.0 * f64(dir_) + 1.0) * hi
    mp = stg[:, unstriped(c2)]
    hid = f64(unit) * (np.minimum(stg, mp) + 0.4 * np.maximum(stg, mp))
    return mxq(f64(w2), 0, "e4m3").T @ mxq(hid, 0, "e4m3")

@@ -1,0 +1,232 @@
+from contextlib import ExitStack
+
+import concourse.mybir as mybir
+
+F32 = mybir.dt.float32
+BF16 = mybir.dt.bfloat16
+I32 = mybir.dt.int32
+U32 = mybir.dt.uint32
+U16 = mybir.dt.uint16
+U8 = mybir.dt.uint8
+FP8X4 = mybir.dt.float8_e4m3fn_x4
+ALU = mybir.AluOpType
+ACT = mybir.ActivationFunctionType
+
+P = 128
+PACK = 4
+T = 1024
+S = 512
+H = 512
+N = 128
+HALF = S // 2
+MIX = 0.4
+FLOPS = 2 * 512 * H * S + 2 * H * N * S
+
+
+def tile_picked_ybitonc_soft_p_kernel(
+    tc, x_words, x_scales, w1, dir_, unit, w2, offs, c1, c2, out
+):
+    nc = tc.nc
+    with ExitStack() as ctx:
+        lists = ctx.enter_context(tc.tile_pool(name="lists", bufs=1))
+        sb = ctx.enter_context(tc.tile_pool(name="sb", bufs=1))
+        psum = ctx.enter_context(tc.psum_pool(name="psum", bufs=1))
+
+        offs_sb = lists.tile([P, S // 16], U16, name="offs_sb")
+        c1_sb = lists.tile([P, S // 16], U16, name="c1_sb")
+        c2_sb = lists.tile([P, S // 16], U16, name="c2_sb")
+
+        def half_cols(hf):
+            return slice(hf * HALF, (hf + 1) * HALF)
+
+        def half_list(list_sb, hf):
+            return list_sb[:, hf * (HALF // 16) : (hf + 1) * (HALF // 16)]
+
+        x_word_table = sb.tile([P, T], I32, name="x_word_table")
+        x_scale_table = sb.tile([P, T], U8, name="x_scale_table")
+        w1_raw = sb.tile([P, PACK, H], F32, name="w1_raw")
+        w2_raw = sb.tile([P, PACK, N], F32, name="w2_raw")
+        unit_sb = sb.tile([P, PACK], F32, name="unit_sb")
+        dirs = [sb.tile([P, S], F32, name=f"dir{t}") for t in range(PACK)]
+
+        nc.vector.memset(x_scale_table[:].bitcast(I32), 0)
+        nc.sync.dma_start(offs_sb[:], offs)
+        nc.sync.dma_start(x_word_table[:], x_words[0].rearrange("p c r -> p (c r)").bitcast(I32))
+        for q in range(4):
+            nc.scalar.dma_start(
+                x_scale_table[32 * q : 32 * q + 4, :].bitcast(I32),
+                x_scales[0, 4 * q : 4 * q + 4, :].bitcast(I32),
+            )
+        nc.sync.dma_start(unit_sb[:], unit.rearrange("(p t) o -> p (t o)", t=PACK))
+        nc.sync.dma_start(w1_raw[:], w1.rearrange("(p j) c -> p j c", j=PACK))
+        nc.sync.dma_start(w2_raw[:], w2.rearrange("(p t) n -> p t n", t=PACK))
+        nc.sync.dma_start(c1_sb[:], c1)
+        dir_planes = dir_.rearrange("(p t) s -> p t s", t=PACK)
+        for t in range(PACK):
+            nc.sync.dma_start(dirs[t][:], dir_planes[:, t, :])
+        nc.sync.dma_start(c2_sb[:], c2)
+
+        unit_abs = sb.tile([P, PACK], F32, name="unit_abs")
+        unit_step = sb.tile([P, PACK], F32, name="unit_step")
+        unit_sign = sb.tile([P, PACK], F32, name="unit_sign")
+        nc.scalar.activation(unit_abs[:], unit_sb[:], ACT.Abs)
+
+        x_codes = sb.tile([P, S], U32, name="x_codes", align_bytes=64)
+        x_bytes = sb.tile([P, S], U8, name="x_bytes", align_bytes=64)
+        nc.vector.tensor_copy(x_bytes[:], x_scale_table[:].indirect(offs_sb[:]))
+        nc.vector.tensor_copy(x_codes[:], x_word_table[:].bitcast(U32).indirect(offs_sb[:]))
+        nc.vector.tensor_scalar(unit_step[:], unit_sb[:], 0.0, 2.0, ALU.is_ge, ALU.mult)
+        nc.vector.tensor_scalar(unit_sign[:], unit_step[:], -1.0, None, ALU.add)
+
+        w1_cols = w1_raw[:].rearrange("p j (m t) -> p m j t", t=PACK)
+        w1_codes = []
+        w1_scales = []
+        for u in range(2):
+            w1_bf = sb.tile([P, 2, P, PACK], BF16, name=f"w1_bf{u}", align_bytes=64)
+            codes = sb.tile([P, 2 * P], U32, name=f"w1_codes{u}", align_bytes=64)
+            scales = sb.tile([P, 2 * P], U8, name=f"w1_scales{u}", align_bytes=64)
+            dst = w1_bf[:].rearrange("p t m j -> p m j t")
+            src = w1_cols[:, :, :, 2 * u : 2 * u + 2]
+            if u == 0:
+                nc.vector.tensor_copy(dst, src)
+            else:
+                nc.scalar.copy(dst, src)
+            nc.vector.quantize_mx(
+                out=codes[:].bitcast(FP8X4),
+                scales=scales[:],
+                in_=w1_bf[:].rearrange("p t m j -> p (t m j)"),
+            )
+            w1_codes.append(codes)
+            w1_scales.append(scales)
+
+        y_banks = [psum.tile([P, S], F32, name=f"y{t}") for t in range(PACK)]
+        for t in range(PACK):
+            cols = slice((t % 2) * P, (t % 2 + 1) * P)
+            nc.tensor.matmul_mx(
+                out=y_banks[t][:],
+                lhsT=w1_codes[t // 2][:, cols].bitcast(FP8X4),
+                lhsT_scale=w1_scales[t // 2][:, cols],
+                rhs=x_codes[:].bitcast(FP8X4),
+                rhs_scale=x_bytes[:],
+                start=True,
+                stop=True,
+            )
+
+        z = [sb.tile([P, S], F32, name=f"z{t}") for t in range(PACK)]
+        zp = [sb.tile([P, S], F32, name=f"zp{t}") for t in range(PACK)]
+        diff = [sb.tile([P, S], F32, name=f"diff{t}") for t in range(PACK)]
+        gap = [sb.tile([P, S], F32, name=f"gap{t}") for t in range(PACK)]
+        hi = [sb.tile([P, S], F32, name=f"hi{t}") for t in range(PACK)]
+        drop = [sb.tile([P, S], F32, name=f"drop{t}") for t in range(PACK)]
+        stg = [sb.tile([P, 2, S], F32, name=f"stg{u}") for u in range(2)]
+        mp = [[sb.tile([P, 2, HALF], F32, name=f"mp{u}{hf}") for hf in range(2)] for u in range(2)]
+        mix_a = [sb.tile([P, 2, HALF, 2], BF16, name=f"mix_a{hf}") for hf in range(2)]
+        mix_b = [sb.tile([P, 2, HALF, 2], BF16, name=f"mix_b{hf}") for hf in range(2)]
+
+        def evacuate(t):
+            nc.scalar.activation(z[t][:], y_banks[t][:], ACT.Copy, scale=unit_abs[:, t : t + 1])
+
+        def partners1(t, hf, on_vector):
+            looked_up = z[t][:].indirect(half_list(c1_sb, hf))
+            if on_vector:
+                nc.vector.tensor_copy(zp[t][:, half_cols(hf)], looked_up)
+            else:
+                nc.scalar.activation(zp[t][:, half_cols(hf)], looked_up, ACT.Copy)
+
+        def difference(t):
+            nc.vector.scalar_tensor_tensor(
+                diff[t][:], y_banks[t][:], unit_abs[:, t : t + 1], zp[t][:], ALU.mult, ALU.subtract
+            )
+
+        def larger(t):
+            nc.vector.scalar_tensor_tensor(
+                hi[t][:], y_banks[t][:], unit_abs[:, t : t + 1], zp[t][:], ALU.mult, ALU.max
+            )
+
+        def magnitude(t):
+            nc.scalar.activation(gap[t][:], diff[t][:], ACT.Abs)
+
+        def weigh(t):
+            nc.vector.tensor_tensor(drop[t][:], gap[t][:], dirs[t][:], ALU.mult)
+
+        def stage1(t):
+            nc.vector.tensor_tensor(stg[t // 2][:, t % 2, :], hi[t][:], drop[t][:], ALU.subtract)
+
+        def partners2(t):
+            for hf in range(2):
+                looked_up = stg[t // 2][:, t % 2, :].indirect(half_list(c2_sb, hf))
+                nc.scalar.activation(mp[t // 2][hf][:, t % 2, :], looked_up, ACT.Copy)
+
+        def mixes(u, hf):
+            own = stg[u][:, :, half_cols(hf)].rearrange("p t c -> p c t")
+            other = mp[u][hf][:].rearrange("p t c -> p c t")
+            nc.vector.scalar_tensor_tensor(mix_a[hf][:, u, :, :], own, MIX, other, ALU.mult, ALU.add)
+            nc.vector.scalar_tensor_tensor(mix_b[hf][:, u, :, :], other, MIX, own, ALU.mult, ALU.add)
+
+        w2_bf = sb.tile([P, N, PACK], BF16, name="w2_bf", align_bytes=64)
+        w2_codes = sb.tile([P, N], U32, name="w2_codes", align_bytes=64)
+        w2_scales = sb.tile([P, N], U8, name="w2_scales", align_bytes=64)
+
+        evacuate(0)
+        nc.vector.tensor_tensor(
+            w2_bf[:].rearrange("p (c i) t -> p c t i", i=4),
+            w2_raw[:].rearrange("p t (c i) -> p c t i", i=4),
+            unit_sign[:].unsqueeze(1).unsqueeze(3).to_broadcast([P, N // 4, PACK, 4]),
+            ALU.mult,
+        )
+        partners1(0, 0, False)
+        partners1(0, 1, True)
+        evacuate(1)
+        difference(0)
+        partners1(1, 0, False)
+        partners1(1, 1, True)
+        magnitude(0)
+        larger(0)
+        nc.vector.quantize_mx(
+            out=w2_codes[:].bitcast(FP8X4), scales=w2_scales[:], in_=w2_bf[:].rearrange("p n t -> p (n t)")
+        )
+        for t in range(1, PACK):
+            difference(t)
+            if t + 1 < PACK:
+                evacuate(t + 1)
+            magnitude(t)
+            if t + 1 < PACK:
+                partners1(t + 1, 0, False)
+                partners1(t + 1, 1, False)
+            weigh(t - 1)
+            larger(t)
+            stage1(t - 1)
+        weigh(PACK - 1)
+        stage1(PACK - 1)
+        for t in range(PACK):
+            partners2(t)
+        for u in range(2):
+            for hf in range(2):
+                mixes(u, hf)
+
+        for hf in range(2):
+            hid = sb.tile([P, HALF, PACK], BF16, name=f"hid{hf}", align_bytes=64)
+            hid_codes = sb.tile([P, HALF], U32, name=f"hid_codes{hf}", align_bytes=64)
+            hid_scales = sb.tile([P, HALF], U8, name=f"hid_scales{hf}", align_bytes=64)
+            nc.vector.tensor_tensor(
+                hid[:].rearrange("p c (u e) -> p c u e", u=2),
+                mix_a[hf][:].rearrange("p u c e -> p c u e"),
+                mix_b[hf][:].rearrange("p u c e -> p c u e"),
+                ALU.min,
+            )
+            nc.vector.quantize_mx(
+                out=hid_codes[:].bitcast(FP8X4), scales=hid_scales[:], in_=hid[:].rearrange("p c t -> p (c t)")
+            )
+            out_bank = psum.tile([P, HALF], F32, name=f"out_bank{hf}")
+            nc.tensor.matmul_mx(
+                out=out_bank[:],
+                lhsT=w2_codes[:].bitcast(FP8X4),
+                lhsT_scale=w2_scales[:],
+                rhs=hid_codes[:].bitcast(FP8X4),
+                rhs_scale=hid_scales[:],
+                start=True,
+                stop=True,
+            )
+            result = sb.tile([P, HALF], F32, name=f"result{hf}")
+            nc.scalar.copy(result[:], out_bank[:])
+            nc.sync.dma_start(out[:, half_cols(hf)], result[:])

@@ -44,7 +44,7 @@ def tile_picked_ybitonc_soft_p_kernel(
 
         x_word_table = sb.tile([P, T], I32, name="x_word_table")
         x_scale_table = sb.tile([P, T], U8, name="x_scale_table")
-        w1_raw = sb.tile([P, PACK, H], F32, name="w1_raw")
+        w1_raw = [sb.tile([P, PACK, H // 2], F32, name=f"w1_raw{hf}") for hf in range(2)]
         w2_raw = sb.tile([P, PACK, N], F32, name="w2_raw")
         unit_sb = sb.tile([P, PACK], F32, name="unit_sb")
         dirs = [sb.tile([P, S], F32, name=f"dir{t}") for t in range(PACK)]
@@ -58,7 +58,9 @@ def tile_picked_ybitonc_soft_p_kernel(
                 x_scales[0, 4 * q : 4 * q + 4, :].bitcast(I32),
             )
         nc.sync.dma_start(unit_sb[:], unit.rearrange("(p t) o -> p (t o)", t=PACK))
-        nc.sync.dma_start(w1_raw[:], w1.rearrange("(p j) c -> p j c", j=PACK))
+        w1_rows = w1.rearrange("(p j) c -> p j c", j=PACK)
+        for hf in range(2):
+            nc.sync.dma_start(w1_raw[hf][:], w1_rows[:, :, hf * (H // 2) : (hf + 1) * (H // 2)])
         nc.sync.dma_start(w2_raw[:], w2.rearrange("(p t) n -> p t n", t=PACK))
         nc.sync.dma_start(c1_sb[:], c1)
         dir_planes = dir_.rearrange("(p t) s -> p t s", t=PACK)
@@ -78,34 +80,26 @@ def tile_picked_ybitonc_soft_p_kernel(
         nc.vector.tensor_scalar(unit_step[:], unit_sb[:], 0.0, 2.0, ALU.is_ge, ALU.mult)
         nc.vector.tensor_scalar(unit_sign[:], unit_step[:], -1.0, None, ALU.add)
 
-        w1_cols = w1_raw[:].rearrange("p j (m t) -> p m j t", t=PACK)
-        w1_codes = []
-        w1_scales = []
-        for u in range(2):
-            w1_bf = sb.tile([P, 2, P, PACK], BF16, name=f"w1_bf{u}", align_bytes=64)
-            codes = sb.tile([P, 2 * P], U32, name=f"w1_codes{u}", align_bytes=64)
-            scales = sb.tile([P, 2 * P], U8, name=f"w1_scales{u}", align_bytes=64)
-            dst = w1_bf[:].rearrange("p t m j -> p m j t")
-            src = w1_cols[:, :, :, 2 * u : 2 * u + 2]
-            if u == 0:
-                nc.vector.tensor_copy(dst, src)
-            else:
-                nc.scalar.copy(dst, src)
-            nc.vector.quantize_mx(
-                out=codes[:].bitcast(FP8X4),
-                scales=scales[:],
-                in_=w1_bf[:].rearrange("p t m j -> p (t m j)"),
-            )
-            w1_codes.append(codes)
-            w1_scales.append(scales)
+        w1_bf = [sb.tile([P, 2, P, PACK], BF16, name=f"w1_bf{u}", align_bytes=64) for u in range(2)]
+        for hf in range(2):
+            w1_cols = w1_raw[hf][:].rearrange("p j (m t) -> p m j t", t=PACK)
+            m_half = slice(hf * (P // 2), (hf + 1) * (P // 2))
+            nc.vector.tensor_copy(w1_bf[0][:, :, m_half, :].rearrange("p t m j -> p m j t"), w1_cols[:, :, :, 0:2])
+            nc.scalar.copy(w1_bf[1][:, :, m_half, :].rearrange("p t m j -> p m j t"), w1_cols[:, :, :, 2:4])
 
         y_banks = [psum.tile([P, S], F32, name=f"y{t}") for t in range(PACK)]
         for t in range(PACK):
-            cols = slice((t % 2) * P, (t % 2 + 1) * P)
+            w1_codes = sb.tile([P, P], U32, name=f"w1_codes{t}", align_bytes=64)
+            w1_scales = sb.tile([P, P], U8, name=f"w1_scales{t}", align_bytes=64)
+            nc.vector.quantize_mx(
+                out=w1_codes[:].bitcast(FP8X4),
+                scales=w1_scales[:],
+                in_=w1_bf[t // 2][:, t % 2, :, :].rearrange("p m j -> p (m j)"),
+            )
             nc.tensor.matmul_mx(
                 out=y_banks[t][:],
-                lhsT=w1_codes[t // 2][:, cols].bitcast(FP8X4),
-                lhsT_scale=w1_scales[t // 2][:, cols],
+                lhsT=w1_codes[:].bitcast(FP8X4),
+                lhsT_scale=w1_scales[:],
                 rhs=x_codes[:].bitcast(FP8X4),
                 rhs_scale=x_bytes[:],
                 start=True,
@@ -119,9 +113,10 @@ def tile_picked_ybitonc_soft_p_kernel(
         hi = [sb.tile([P, S], F32, name=f"hi{t}") for t in range(PACK)]
         drop = [sb.tile([P, S], F32, name=f"drop{t}") for t in range(PACK)]
         stg = [sb.tile([P, 2, S], F32, name=f"stg{u}") for u in range(2)]
-        mp = [[sb.tile([P, 2, HALF], F32, name=f"mp{u}{hf}") for hf in range(2)] for u in range(2)]
-        mix_a = [sb.tile([P, 2, HALF, 2], BF16, name=f"mix_a{hf}") for hf in range(2)]
-        mix_b = [sb.tile([P, 2, HALF, 2], BF16, name=f"mix_b{hf}") for hf in range(2)]
+        chunks = [(0, 256), (256, 128), (384, 128)]
+        mp = [[sb.tile([P, 2, w], F32, name=f"mp{u}{ci}") for ci, (c0, w) in enumerate(chunks)] for u in range(2)]
+        mix_a = [sb.tile([P, 2, w, 2], BF16, name=f"mix_a{ci}") for ci, (c0, w) in enumerate(chunks)]
+        mix_b = [sb.tile([P, 2, w, 2], BF16, name=f"mix_b{ci}") for ci, (c0, w) in enumerate(chunks)]
 
         def evacuate(t):
             nc.scalar.activation(z[t][:], y_banks[t][:], ACT.Copy, scale=unit_abs[:, t : t + 1])
@@ -147,21 +142,22 @@ def tile_picked_ybitonc_soft_p_kernel(
             nc.scalar.activation(gap[t][:], diff[t][:], ACT.Abs)
 
         def weigh(t):
-            nc.vector.tensor_tensor(drop[t][:], gap[t][:], dirs[t][:], ALU.mult)
+            nc.gpsimd.tensor_tensor(drop[t][:], gap[t][:], dirs[t][:], ALU.mult)
 
         def stage1(t):
             nc.vector.tensor_tensor(stg[t // 2][:, t % 2, :], hi[t][:], drop[t][:], ALU.subtract)
 
         def partners2(t):
-            for hf in range(2):
-                looked_up = stg[t // 2][:, t % 2, :].indirect(half_list(c2_sb, hf))
-                nc.scalar.activation(mp[t // 2][hf][:, t % 2, :], looked_up, ACT.Copy)
+            for ci, (c0, w) in enumerate(chunks):
+                looked_up = stg[t // 2][:, t % 2, :].indirect(c2_sb[:, c0 // 16 : (c0 + w) // 16])
+                nc.scalar.activation(mp[t // 2][ci][:, t % 2, :], looked_up, ACT.Copy)
 
-        def mixes(u, hf):
-            own = stg[u][:, :, half_cols(hf)].rearrange("p t c -> p c t")
-            other = mp[u][hf][:].rearrange("p t c -> p c t")
-            nc.vector.scalar_tensor_tensor(mix_a[hf][:, u, :, :], own, MIX, other, ALU.mult, ALU.add)
-            nc.vector.scalar_tensor_tensor(mix_b[hf][:, u, :, :], other, MIX, own, ALU.mult, ALU.add)
+        def mixes(u, ci):
+            c0, w = chunks[ci]
+            own = stg[u][:, :, c0 : c0 + w].rearrange("p t c -> p c t")
+            other = mp[u][ci][:].rearrange("p t c -> p c t")
+            nc.vector.scalar_tensor_tensor(mix_a[ci][:, u, :, :], own, MIX, other, ALU.mult, ALU.add)
+            nc.vector.scalar_tensor_tensor(mix_b[ci][:, u, :, :], other, MIX, own, ALU.mult, ALU.add)
 
         w2_bf = sb.tile([P, N, PACK], BF16, name="w2_bf", align_bytes=64)
         w2_codes = sb.tile([P, N], U32, name="w2_codes", align_bytes=64)
@@ -177,47 +173,43 @@ def tile_picked_ybitonc_soft_p_kernel(
         partners1(0, 0, False)
         partners1(0, 1, True)
         evacuate(1)
-        difference(0)
-        partners1(1, 0, False)
-        partners1(1, 1, True)
-        magnitude(0)
-        larger(0)
-        nc.vector.quantize_mx(
-            out=w2_codes[:].bitcast(FP8X4), scales=w2_scales[:], in_=w2_bf[:].rearrange("p n t -> p (n t)")
-        )
-        for t in range(1, PACK):
+        for t in range(PACK):
             difference(t)
-            if t + 1 < PACK:
-                evacuate(t + 1)
             magnitude(t)
+            if t > 0:
+                stage1(t - 1)
+            weigh(t)
+            larger(t)
             if t + 1 < PACK:
                 partners1(t + 1, 0, False)
-                partners1(t + 1, 1, False)
-            weigh(t - 1)
-            larger(t)
-            stage1(t - 1)
-        weigh(PACK - 1)
+                partners1(t + 1, 1, True)
+            if t + 2 < PACK:
+                evacuate(t + 2)
         stage1(PACK - 1)
         for t in range(PACK):
             partners2(t)
-        for u in range(2):
-            for hf in range(2):
-                mixes(u, hf)
+        nc.vector.quantize_mx(
+            out=w2_codes[:].bitcast(FP8X4), scales=w2_scales[:], in_=w2_bf[:].rearrange("p n t -> p (n t)")
+        )
 
-        for hf in range(2):
-            hid = sb.tile([P, HALF, PACK], BF16, name=f"hid{hf}", align_bytes=64)
-            hid_codes = sb.tile([P, HALF], U32, name=f"hid_codes{hf}", align_bytes=64)
-            hid_scales = sb.tile([P, HALF], U8, name=f"hid_scales{hf}", align_bytes=64)
+        hid = [sb.tile([P, w, PACK], BF16, name=f"hid{ci}", align_bytes=64) for ci, (c0, w) in enumerate(chunks)]
+
+        def smaller(ci):
             nc.vector.tensor_tensor(
-                hid[:].rearrange("p c (u e) -> p c u e", u=2),
-                mix_a[hf][:].rearrange("p u c e -> p c u e"),
-                mix_b[hf][:].rearrange("p u c e -> p c u e"),
+                hid[ci][:].rearrange("p c (u e) -> p c u e", u=2),
+                mix_a[ci][:].rearrange("p u c e -> p c u e"),
+                mix_b[ci][:].rearrange("p u c e -> p c u e"),
                 ALU.min,
             )
+
+        def product2(ci):
+            c0, w = chunks[ci]
+            hid_codes = sb.tile([P, w], U32, name=f"hid_codes{ci}", align_bytes=64)
+            hid_scales = sb.tile([P, w], U8, name=f"hid_scales{ci}", align_bytes=64)
             nc.vector.quantize_mx(
-                out=hid_codes[:].bitcast(FP8X4), scales=hid_scales[:], in_=hid[:].rearrange("p c t -> p (c t)")
+                out=hid_codes[:].bitcast(FP8X4), scales=hid_scales[:], in_=hid[ci][:].rearrange("p c t -> p (c t)")
             )
-            out_bank = psum.tile([P, HALF], F32, name=f"out_bank{hf}")
+            out_bank = psum.tile([P, w], F32, name=f"out_bank{ci}")
             nc.tensor.matmul_mx(
                 out=out_bank[:],
                 lhsT=w2_codes[:].bitcast(FP8X4),
@@ -227,6 +219,15 @@ def tile_picked_ybitonc_soft_p_kernel(
                 start=True,
                 stop=True,
             )
-            result = sb.tile([P, HALF], F32, name=f"result{hf}")
+            result = sb.tile([P, w], F32, name=f"result{ci}")
             nc.scalar.copy(result[:], out_bank[:])
-            nc.sync.dma_start(out[:, half_cols(hf)], result[:])
+            nc.sync.dma_start(out[:, c0 : c0 + w], result[:])
+
+        for ci in range(len(chunks)):
+            mixes(0, ci)
+        for ci in range(len(chunks)):
+            mixes(1, ci)
+            if ci > 0:
+                product2(ci - 1)
+            smaller(ci)
+        product2(len(chunks) - 1)

@@ -50,17 +50,17 @@ def tile_picked_ybitonc_soft_p_kernel(
         dirs = [sb.tile([P, S], F32, name=f"dir{t}") for t in range(PACK)]
 
         nc.vector.memset(x_scale_table[:].bitcast(I32), 0)
-        nc.sync.dma_start(offs_sb[:], offs)
         nc.sync.dma_start(x_word_table[:], x_words[0].rearrange("p c r -> p (c r)").bitcast(I32))
         for q in range(4):
-            nc.scalar.dma_start(
+            nc.sync.dma_start(
                 x_scale_table[32 * q : 32 * q + 4, :].bitcast(I32),
                 x_scales[0, 4 * q : 4 * q + 4, :].bitcast(I32),
             )
-        nc.sync.dma_start(unit_sb[:], unit.rearrange("(p t) o -> p (t o)", t=PACK))
+        nc.sync.dma_start(offs_sb[:], offs)
         w1_rows = w1.rearrange("(p j) c -> p j c", j=PACK)
         for hf in range(2):
             nc.sync.dma_start(w1_raw[hf][:], w1_rows[:, :, hf * (H // 2) : (hf + 1) * (H // 2)])
+        nc.sync.dma_start(unit_sb[:], unit.rearrange("(p t) o -> p (t o)", t=PACK))
         nc.sync.dma_start(w2_raw[:], w2.rearrange("(p t) n -> p t n", t=PACK))
         nc.sync.dma_start(c1_sb[:], c1)
         dir_planes = dir_.rearrange("(p t) s -> p t s", t=PACK)
@@ -75,8 +75,8 @@ def tile_picked_ybitonc_soft_p_kernel(
 
         x_codes = sb.tile([P, S], U32, name="x_codes", align_bytes=64)
         x_bytes = sb.tile([P, S], U8, name="x_bytes", align_bytes=64)
-        nc.vector.tensor_copy(x_bytes[:], x_scale_table[:].indirect(offs_sb[:]))
         nc.vector.tensor_copy(x_codes[:], x_word_table[:].bitcast(U32).indirect(offs_sb[:]))
+        nc.vector.tensor_copy(x_bytes[:], x_scale_table[:].indirect(offs_sb[:]))
         nc.vector.tensor_scalar(unit_step[:], unit_sb[:], 0.0, 2.0, ALU.is_ge, ALU.mult)
         nc.vector.tensor_scalar(unit_sign[:], unit_step[:], -1.0, None, ALU.add)
 
@@ -119,7 +119,10 @@ def tile_picked_ybitonc_soft_p_kernel(
         mix_b = [sb.tile([P, 2, w, 2], BF16, name=f"mix_b{ci}") for ci, (c0, w) in enumerate(chunks)]
 
         def evacuate(t):
-            nc.scalar.activation(z[t][:], y_banks[t][:], ACT.Copy, scale=unit_abs[:, t : t + 1])
+            if t == 1:
+                nc.vector.tensor_scalar(z[t][:], y_banks[t][:], unit_abs[:, t : t + 1], None, ALU.mult)
+            else:
+                nc.scalar.activation(z[t][:], y_banks[t][:], ACT.Copy, scale=unit_abs[:, t : t + 1])
 
         def partners1(t, hf, on_vector):
             looked_up = z[t][:].indirect(half_list(c1_sb, hf))
@@ -142,7 +145,7 @@ def tile_picked_ybitonc_soft_p_kernel(
             nc.scalar.activation(gap[t][:], diff[t][:], ACT.Abs)
 
         def weigh(t):
-            nc.gpsimd.tensor_tensor(drop[t][:], gap[t][:], dirs[t][:], ALU.mult)
+            nc.vector.tensor_tensor(drop[t][:], gap[t][:], dirs[t][:], ALU.mult)
 
         def stage1(t):
             nc.vector.tensor_tensor(stg[t // 2][:, t % 2, :], hi[t][:], drop[t][:], ALU.subtract)
@@ -170,27 +173,31 @@ def tile_picked_ybitonc_soft_p_kernel(
             unit_sign[:].unsqueeze(1).unsqueeze(3).to_broadcast([P, N // 4, PACK, 4]),
             ALU.mult,
         )
-        partners1(0, 0, False)
-        partners1(0, 1, True)
-        evacuate(1)
-        for t in range(PACK):
-            difference(t)
-            magnitude(t)
-            if t > 0:
-                stage1(t - 1)
-            weigh(t)
-            larger(t)
-            if t + 1 < PACK:
-                partners1(t + 1, 0, False)
-                partners1(t + 1, 1, True)
-            if t + 2 < PACK:
-                evacuate(t + 2)
-        stage1(PACK - 1)
-        for t in range(PACK):
-            partners2(t)
         nc.vector.quantize_mx(
             out=w2_codes[:].bitcast(FP8X4), scales=w2_scales[:], in_=w2_bf[:].rearrange("p n t -> p (n t)")
         )
+        evacuate(1)
+        for t in range(2):
+            partners1(t, 0, False)
+            partners1(t, 1, True)
+        for t in range(PACK):
+            difference(t)
+            if t >= 2:
+                stage1(t - 2)
+            larger(t)
+            if t >= 1:
+                weigh(t - 1)
+            if t + 2 < PACK:
+                evacuate(t + 2)
+            magnitude(t)
+            if t + 2 < PACK:
+                partners1(t + 2, 0, False)
+                partners1(t + 2, 1, False)
+        stage1(PACK - 2)
+        weigh(PACK - 1)
+        stage1(PACK - 1)
+        for t in range(PACK):
+            partners2(t)
 
         hid = [sb.tile([P, w, PACK], BF16, name=f"hid{ci}", align_bytes=64) for ci, (c0, w) in enumerate(chunks)]
 
@@ -225,9 +232,12 @@ def tile_picked_ybitonc_soft_p_kernel(
 
         for ci in range(len(chunks)):
             mixes(0, ci)
-        for ci in range(len(chunks)):
-            mixes(1, ci)
-            if ci > 0:
-                product2(ci - 1)
-            smaller(ci)
-        product2(len(chunks) - 1)
+        mixes(1, 0)
+        mixes(1, 1)
+        smaller(0)
+        mixes(1, 2)
+        product2(0)
+        smaller(1)
+        smaller(2)
+        product2(1)
+        product2(2)

from contextlib import ExitStack

import concourse.mybir as mybir

F32 = mybir.dt.float32
BF16 = mybir.dt.bfloat16
I32 = mybir.dt.int32
U32 = mybir.dt.uint32
U16 = mybir.dt.uint16
U8 = mybir.dt.uint8
FP8X4 = mybir.dt.float8_e4m3fn_x4
ALU = mybir.AluOpType
ACT = mybir.ActivationFunctionType

P = 128
PACK = 4
T = 1024
S = 512
H = 512
N = 128
HALF = S // 2
MIX = 0.4
FLOPS = 2 * 512 * H * S + 2 * H * N * S


def tile_picked_ybitonc_soft_p_kernel(
    tc, x_words, x_scales, w1, dir_, unit, w2, offs, c1, c2, out
):
    nc = tc.nc
    with ExitStack() as ctx:
        lists = ctx.enter_context(tc.tile_pool(name="lists", bufs=1))
        sb = ctx.enter_context(tc.tile_pool(name="sb", bufs=1))
        psum = ctx.enter_context(tc.psum_pool(name="psum", bufs=1))

        offs_sb = lists.tile([P, S // 16], U16, name="offs_sb")
        c1_sb = lists.tile([P, S // 16], U16, name="c1_sb")
        c2_sb = lists.tile([P, S // 16], U16, name="c2_sb")

        def half_cols(hf):
            return slice(hf * HALF, (hf + 1) * HALF)

        def half_list(list_sb, hf):
            return list_sb[:, hf * (HALF // 16) : (hf + 1) * (HALF // 16)]

        x_word_table = sb.tile([P, T], I32, name="x_word_table")
        x_scale_table = sb.tile([P, T], U8, name="x_scale_table")
        w1_raw = [sb.tile([P, PACK, H // 2], F32, name=f"w1_raw{hf}") for hf in range(2)]
        w2_raw = sb.tile([P, PACK, N], F32, name="w2_raw")
        unit_sb = sb.tile([P, PACK], F32, name="unit_sb")
        dirs = [sb.tile([P, S], F32, name=f"dir{t}") for t in range(PACK)]

        nc.vector.memset(x_scale_table[:].bitcast(I32), 0)
        nc.sync.dma_start(x_word_table[:], x_words[0].rearrange("p c r -> p (c r)").bitcast(I32))
        for q in range(4):
            nc.sync.dma_start(
                x_scale_table[32 * q : 32 * q + 4, :].bitcast(I32),
                x_scales[0, 4 * q : 4 * q + 4, :].bitcast(I32),
            )
        nc.sync.dma_start(offs_sb[:], offs)
        w1_rows = w1.rearrange("(p j) c -> p j c", j=PACK)
        for hf in range(2):
            nc.sync.dma_start(w1_raw[hf][:], w1_rows[:, :, hf * (H // 2) : (hf + 1) * (H // 2)])
        nc.sync.dma_start(unit_sb[:], unit.rearrange("(p t) o -> p (t o)", t=PACK))
        nc.sync.dma_start(w2_raw[:], w2.rearrange("(p t) n -> p t n", t=PACK))
        nc.sync.dma_start(c1_sb[:], c1)
        dir_planes = dir_.rearrange("(p t) s -> p t s", t=PACK)
        for t in range(PACK):
            nc.sync.dma_start(dirs[t][:], dir_planes[:, t, :])
        nc.sync.dma_start(c2_sb[:], c2)

        unit_abs = sb.tile([P, PACK], F32, name="unit_abs")
        unit_step = sb.tile([P, PACK], F32, name="unit_step")
        unit_sign = sb.tile([P, PACK], F32, name="unit_sign")
        nc.scalar.activation(unit_abs[:], unit_sb[:], ACT.Abs)

        x_codes = sb.tile([P, S], U32, name="x_codes", align_bytes=64)
        x_bytes = sb.tile([P, S], U8, name="x_bytes", align_bytes=64)
        nc.vector.tensor_copy(x_codes[:], x_word_table[:].bitcast(U32).indirect(offs_sb[:]))
        nc.vector.tensor_copy(x_bytes[:], x_scale_table[:].indirect(offs_sb[:]))
        nc.vector.tensor_scalar(unit_step[:], unit_sb[:], 0.0, 2.0, ALU.is_ge, ALU.mult)
        nc.vector.tensor_scalar(unit_sign[:], unit_step[:], -1.0, None, ALU.add)

        w1_bf = [sb.tile([P, 2, P, PACK], BF16, name=f"w1_bf{u}", align_bytes=64) for u in range(2)]
        for hf in range(2):
            w1_cols = w1_raw[hf][:].rearrange("p j (m t) -> p m j t", t=PACK)
            m_half = slice(hf * (P // 2), (hf + 1) * (P // 2))
            nc.vector.tensor_copy(w1_bf[0][:, :, m_half, :].rearrange("p t m j -> p m j t"), w1_cols[:, :, :, 0:2])
            nc.scalar.copy(w1_bf[1][:, :, m_half, :].rearrange("p t m j -> p m j t"), w1_cols[:, :, :, 2:4])

        y_banks = [psum.tile([P, S], F32, name=f"y{t}") for t in range(PACK)]
        for t in range(PACK):
            w1_codes = sb.tile([P, P], U32, name=f"w1_codes{t}", align_bytes=64)
            w1_scales = sb.tile([P, P], U8, name=f"w1_scales{t}", align_bytes=64)
            nc.vector.quantize_mx(
                out=w1_codes[:].bitcast(FP8X4),
                scales=w1_scales[:],
                in_=w1_bf[t // 2][:, t % 2, :, :].rearrange("p m j -> p (m j)"),
            )
            nc.tensor.matmul_mx(
                out=y_banks[t][:],
                lhsT=w1_codes[:].bitcast(FP8X4),
                lhsT_scale=w1_scales[:],
                rhs=x_codes[:].bitcast(FP8X4),
                rhs_scale=x_bytes[:],
                start=True,
                stop=True,
            )

        z = [sb.tile([P, S], F32, name=f"z{t}") for t in range(PACK)]
        zp = [sb.tile([P, S], F32, name=f"zp{t}") for t in range(PACK)]
        diff = [sb.tile([P, S], F32, name=f"diff{t}") for t in range(PACK)]
        gap = [sb.tile([P, S], F32, name=f"gap{t}") for t in range(PACK)]
        hi = [sb.tile([P, S], F32, name=f"hi{t}") for t in range(PACK)]
        drop = [sb.tile([P, S], F32, name=f"drop{t}") for t in range(PACK)]
        stg = [sb.tile([P, 2, S], F32, name=f"stg{u}") for u in range(2)]
        chunks = [(0, 256), (256, 128), (384, 128)]
        mp = [[sb.tile([P, 2, w], F32, name=f"mp{u}{ci}") for ci, (c0, w) in enumerate(chunks)] for u in range(2)]
        mix_a = [sb.tile([P, 2, w, 2], BF16, name=f"mix_a{ci}") for ci, (c0, w) in enumerate(chunks)]
        mix_b = [sb.tile([P, 2, w, 2], BF16, name=f"mix_b{ci}") for ci, (c0, w) in enumerate(chunks)]

        def evacuate(t):
            if t == 1:
                nc.vector.tensor_scalar(z[t][:], y_banks[t][:], unit_abs[:, t : t + 1], None, ALU.mult)
            else:
                nc.scalar.activation(z[t][:], y_banks[t][:], ACT.Copy, scale=unit_abs[:, t : t + 1])

        def partners1(t, hf, on_vector):
            looked_up = z[t][:].indirect(half_list(c1_sb, hf))
            if on_vector:
                nc.vector.tensor_copy(zp[t][:, half_cols(hf)], looked_up)
            else:
                nc.scalar.activation(zp[t][:, half_cols(hf)], looked_up, ACT.Copy)

        def difference(t):
            nc.vector.scalar_tensor_tensor(
                diff[t][:], y_banks[t][:], unit_abs[:, t : t + 1], zp[t][:], ALU.mult, ALU.subtract
            )

        def larger(t):
            nc.vector.scalar_tensor_tensor(
                hi[t][:], y_banks[t][:], unit_abs[:, t : t + 1], zp[t][:], ALU.mult, ALU.max
            )

        def magnitude(t):
            nc.scalar.activation(gap[t][:], diff[t][:], ACT.Abs)

        def weigh(t):
            nc.vector.tensor_tensor(drop[t][:], gap[t][:], dirs[t][:], ALU.mult)

        def stage1(t):
            nc.vector.tensor_tensor(stg[t // 2][:, t % 2, :], hi[t][:], drop[t][:], ALU.subtract)

        def partners2(t):
            for ci, (c0, w) in enumerate(chunks):
                looked_up = stg[t // 2][:, t % 2, :].indirect(c2_sb[:, c0 // 16 : (c0 + w) // 16])
                nc.scalar.activation(mp[t // 2][ci][:, t % 2, :], looked_up, ACT.Copy)

        def mixes(u, ci):
            c0, w = chunks[ci]
            own = stg[u][:, :, c0 : c0 + w].rearrange("p t c -> p c t")
            other = mp[u][ci][:].rearrange("p t c -> p c t")
            nc.vector.scalar_tensor_tensor(mix_a[ci][:, u, :, :], own, MIX, other, ALU.mult, ALU.add)
            nc.vector.scalar_tensor_tensor(mix_b[ci][:, u, :, :], other, MIX, own, ALU.mult, ALU.add)

        w2_bf = sb.tile([P, N, PACK], BF16, name="w2_bf", align_bytes=64)
        w2_codes = sb.tile([P, N], U32, name="w2_codes", align_bytes=64)
        w2_scales = sb.tile([P, N], U8, name="w2_scales", align_bytes=64)

        evacuate(0)
        nc.vector.tensor_tensor(
            w2_bf[:].rearrange("p (c i) t -> p c t i", i=4),
            w2_raw[:].rearrange("p t (c i) -> p c t i", i=4),
            unit_sign[:].unsqueeze(1).unsqueeze(3).to_broadcast([P, N // 4, PACK, 4]),
            ALU.mult,
        )
        nc.vector.quantize_mx(
            out=w2_codes[:].bitcast(FP8X4), scales=w2_scales[:], in_=w2_bf[:].rearrange("p n t -> p (n t)")
        )
        evacuate(1)
        for t in range(2):
            partners1(t, 0, False)
            partners1(t, 1, True)
        for t in range(PACK):
            difference(t)
            if t >= 2:
                stage1(t - 2)
            larger(t)
            if t >= 1:
                weigh(t - 1)
            if t + 2 < PACK:
                evacuate(t + 2)
            magnitude(t)
            if t + 2 < PACK:
                partners1(t + 2, 0, False)
                partners1(t + 2, 1, False)
        stage1(PACK - 2)
        weigh(PACK - 1)
        stage1(PACK - 1)
        for t in range(PACK):
            partners2(t)

        hid = [sb.tile([P, w, PACK], BF16, name=f"hid{ci}", align_bytes=64) for ci, (c0, w) in enumerate(chunks)]

        def smaller(ci):
            nc.vector.tensor_tensor(
                hid[ci][:].rearrange("p c (u e) -> p c u e", u=2),
                mix_a[ci][:].rearrange("p u c e -> p c u e"),
                mix_b[ci][:].rearrange("p u c e -> p c u e"),
                ALU.min,
            )

        def product2(ci):
            c0, w = chunks[ci]
            hid_codes = sb.tile([P, w], U32, name=f"hid_codes{ci}", align_bytes=64)
            hid_scales = sb.tile([P, w], U8, name=f"hid_scales{ci}", align_bytes=64)
            nc.vector.quantize_mx(
                out=hid_codes[:].bitcast(FP8X4), scales=hid_scales[:], in_=hid[ci][:].rearrange("p c t -> p (c t)")
            )
            out_bank = psum.tile([P, w], F32, name=f"out_bank{ci}")
            nc.tensor.matmul_mx(
                out=out_bank[:],
                lhsT=w2_codes[:].bitcast(FP8X4),
                lhsT_scale=w2_scales[:],
                rhs=hid_codes[:].bitcast(FP8X4),
                rhs_scale=hid_scales[:],
                start=True,
                stop=True,
            )
            result = sb.tile([P, w], F32, name=f"result{ci}")
            nc.scalar.copy(result[:], out_bank[:])
            nc.sync.dma_start(out[:, c0 : c0 + w], result[:])

        for ci in range(len(chunks)):
            mixes(0, ci)
        mixes(1, 0)
        mixes(1, 1)
        smaller(0)
        mixes(1, 2)
        product2(0)
        smaller(1)
        smaller(2)
        product2(1)
        product2(2)
